import numpy as np, ml_dtypes
CORES = [34,162,290,418,42,426]
N = 6
F = 32
def setup_inputs(rng):
    return {"a": rng.standard_normal((N, 128, 128), dtype=np.float32).astype(ml_dtypes.bfloat16), "b": rng.standard_normal((N, 128, F), dtype=np.float32).astype(ml_dtypes.bfloat16)}
def setup_inputs_big(rng):
    d = setup_inputs(rng)
    for k in ("a", "b"): d[k] = (d[k].astype(np.float32) * 1024.0).astype(d[k].dtype)
    return d
def setup_inputs_small(rng):
    d = setup_inputs(rng)
    for k in ("a", "b"): d[k] = (d[k].astype(np.float32) * (1 / 1024.0)).astype(d[k].dtype)
    return d
def setup_inputs_apart(rng):
    d = setup_inputs(rng)
    f = (10.0 ** rng.permutation(np.linspace(-1.5, 1.5, N))).astype(np.float32).reshape(N, 1, 1)
    for k in ("a", "b"): d[k] = (d[k].astype(np.float32) * f).astype(d[k].dtype)
    return d
def reference(a, b):
    s = (a.astype(np.float64).sum(axis=0).T @ b.astype(np.float64).sum(axis=0)).astype(ml_dtypes.bfloat16 if a.dtype != np.float64 else np.float64)
    return {"y": np.broadcast_to(s, (N,) + s.shape)}

from concourse.bass import DstId, RemoteDMATransfer
from concourse.mybir import dt, AluOpType

KA = 128
W = 160
NF = 32

SCRATCH = {
    "own": ("sbuf", [128, W], "bfloat16"),
    "peer0": ("sbuf", [128, W], "bfloat16"),
    "peer1": ("sbuf", [128, W], "bfloat16"),
    "far": ("sbuf", [128, W], "bfloat16"),
    "part": ("sbuf", [128, W], "bfloat16"),
    "mine": ("sbuf", [128, W], "bfloat16"),
    "yb": ("sbuf", [128, NF], "bfloat16"),
    "acc": ("psum", [128, NF], "float32"),
}
SEMAPHORES = ["loaded", "hop1", "hop2", "sent", "added", "summed", "product", "rounded", "stored"]


def _bits(mask):
    return bin(mask).count("1")


def _rack_of(topo, c):
    return topo.rack(topo.host(c))


def _peers(topo, cores, c):
    return [d for d in cores if d != c and _rack_of(topo, d) == _rack_of(topo, c)]


def _peer_mask(topo, cores, c):
    m = -1
    for d in _peers(topo, cores, c):
        m &= topo.mask(c, d)
    return m


def _partner(topo, cores, c):
    return [d for d in cores if _rack_of(topo, d) != _rack_of(topo, c)
            and topo.may_write(c, d) and topo.chip(d) == topo.chip(c)][0]


def rank_program(g, core, T, topo):
    if T.rank_of(core) is None:
        return
    cores = list(T.cores)
    sem = T.sem
    peers = _peers(topo, cores, core)
    partner = _partner(topo, cores, core)
    lands = [T.peer0, T.peer1]

    g.sync.dma_start(T.own[:, 0:KA], T.a[:, :]).then_inc(sem.loaded, 16)
    g.scalar.dma_start(T.own[:, KA:W], T.b[:, :]).then_inc(sem.loaded, 16)

    ids, dsts = [], []
    for d in peers:
        rid, pid = topo.addr(d, core)
        ids.append(DstId(rid=rid, pnc=pid))
        dsts.append(lands[_peers(topo, cores, d).index(core)][:])
    m1 = _peer_mask(topo, cores, core)
    g.wait_ge(sem.loaded, 32)
    g.remote_dma_fused([RemoteDMATransfer(dst_ids=ids, dma_engine_mask=m1, remote_sem=sem.hop1,
                                          srcs=[T.own[:]], dsts=dsts, alu_op=0)], local_sem=sem.sent)
    in1 = sum(_bits(_peer_mask(topo, cores, p)) for p in peers)

    rid, pid = topo.addr(partner, core)
    m2 = topo.mask(core, partner)
    g.wait_ge(sem.hop1, in1)
    g.remote_dma_fused([RemoteDMATransfer(dst_ids=[DstId(rid=rid, pnc=pid)], dma_engine_mask=m2, remote_sem=sem.hop2,
                                          srcs=[T.own[:], T.peer0[:], T.peer1[:]], dsts=[T.far[:]], alu_op=1)],
                       local_sem=sem.sent)
    in2 = _bits(topo.mask(partner, core))

    g.vector.wait_ge(sem.loaded, 32)
    g.vector.wait_ge(sem.hop1, in1)
    g.vector.tensor_tensor(T.part[:], T.own[:], T.peer0[:], AluOpType.add).then_inc(sem.added, 1)
    g.vector.wait_ge(sem.added, 1)
    g.vector.tensor_tensor(T.mine[:], T.part[:], T.peer1[:], AluOpType.add).then_inc(sem.summed, 1)

    g.tensor.wait_ge(sem.summed, 1)
    g.tensor.matmul(T.acc[:], T.mine[:, 0:KA], T.mine[:, KA:W], True, False)
    g.tensor.wait_ge(sem.hop2, in2)
    g.tensor.matmul(T.acc[:], T.mine[:, 0:KA], T.far[:, KA:W], False, False)
    g.tensor.matmul(T.acc[:], T.far[:, 0:KA], T.mine[:, KA:W], False, False)
    g.tensor.matmul(T.acc[:], T.far[:, 0:KA], T.far[:, KA:W], False, True).then_inc(sem.product, 1)

    g.vector.wait_ge(sem.product, 1)
    g.vector.tensor_copy(T.yb[:], T.acc[:]).then_inc(sem.rounded, 1)

    g.sync.wait_ge(sem.rounded, 1)
    g.sync.dma_start(T.y[:, :], T.yb[:]).then_inc(sem.stored, 16)
    g.sync.wait_ge(sem.stored, 16)

    g.wait_ge(sem.sent, _bits(m1) + _bits(m2))
